import numpy as np
import ml_dtypes


def mxq(x, axis, fmt="e4m3"):
    dtype, down = {"e4m3": (ml_dtypes.float8_e4m3fn, 7), "e5m2": (ml_dtypes.float8_e5m2, 14)}[fmt]
    v = np.moveaxis(np.asarray(x, np.float32).astype(ml_dtypes.bfloat16).astype(np.float64), axis, -1)
    blocks = v.reshape(v.shape[:-1] + (-1, 32))
    amax = np.abs(blocks).max(-1, keepdims=True)
    byte = np.maximum(np.where(amax > 0, np.frexp(amax)[1] - 1 + 127, 0) - down, 1)
    scale = np.exp2(byte - 127.0)
    codes = (blocks / scale).astype(np.float32).astype(dtype).astype(np.float64)
    return np.moveaxis((codes * scale).reshape(v.shape), -1, axis)


WIDE = False


def mx_kscale(k):
    if not WIDE:
        return np.ones(k)
    levels = np.array([10, -10, 5, -5, 0])
    if k % 512:
        return np.exp2(np.random.permutation(np.resize(levels, k // 32))).repeat(32)
    a = np.empty((k // 512, 16))
    for p in range(k // 512):
        a[p, :8] = np.random.permutation(np.resize(levels, 8))
        for g in range(8):
            far = levels[np.abs(levels - a[p, g]) >= 10]
            a[p, g + 8] = far[np.random.randint(len(far))]
    return np.exp2(a.ravel()).repeat(32)


def f64(x):
    return np.asarray(x).astype(np.float64)


def striped(idx):
    return np.tile(idx.reshape(-1, 16).T, (8, 1)).astype(np.uint16)


def unstriped(offs):
    return offs[:16].T.reshape(-1).astype(np.int64)


def pack_weight(w):
    k, n = w.shape
    w = f64(np.asarray(w, np.float32).astype(ml_dtypes.bfloat16)).reshape(k // 32, 32, n)
    amax = np.abs(w).max(1)
    byte = np.clip(np.where(amax > 0, np.frexp(amax)[1] - 1 + 127 - 7, 1), 1, 254)
    scaled = (w * np.exp2(127.0 - byte)[:, None, :]).reshape(k, n).astype(np.float32)
    words = np.ascontiguousarray(scaled.reshape(k // 512, 128, 4, n).transpose(0, 1, 3, 2)).astype(ml_dtypes.float8_e4m3fn).view(np.uint8)
    return words, np.ascontiguousarray(byte.astype(np.uint8).reshape(k // 512, 16, n))


def unpack_weight(words, scales):
    g, p, n, _ = words.shape
    vals = np.ascontiguousarray(words).view(ml_dtypes.float8_e4m3fn).astype(np.float64) * np.repeat(np.exp2(scales.astype(np.float64) - 127.0), 8, axis=1)[..., None]
    return vals.transpose(0, 1, 3, 2).reshape(g * 512, n)


K, T, S, N, H = 1024, 2048, 512, 128, 512


def setup_inputs():
    n = np.random.standard_normal
    s = mx_kscale(K)[:, None]
    u = mx_kscale(H)
    packed_xT = pack_weight(n((K, T)) * s)
    return {
        "x_words": packed_xT[0],
        "x_scales": packed_xT[1],
        "w1": (n((K, H)) / np.sqrt(K) / s).astype(np.float32),
        "w2": (n((K, H)) / np.sqrt(K) / s).astype(np.float32),
        "unit": (np.random.uniform(0.6, 1.4, (H, 1)) * u[:, None]).astype(np.float32),
        "w3": (n((H, N)) / np.sqrt(H) / u[:, None]).astype(np.float32),
        "offs": striped(np.random.permutation(T)[:S]),
        "cle": striped(np.random.permutation(S)),
        "cr2": striped(np.random.permutation(S)),
    }


def reference(x_words, x_scales, w1, w2, unit, w3, offs, cle, cr2):
    xq = unpack_weight(x_words, x_scales)[:, unstriped(offs)]
    y = mxq(f64(w1), 0, "e4m3").T @ xq
    z1 = mxq(f64(w2), 0, "e4m3").T @ xq
    zc = z1[:, unstriped(cle)]
    sum_ = y + 0.7 * zc
    s2 = sum_[:, unstriped(cr2)]
    yk2 = y[:, unstriped(cr2)]
    hid = f64(unit) * (s2 + yk2)
    return mxq(f64(w3), 0, "e4m3").T @ mxq(hid, 0, "e4m3")

@@ -1,0 +1,208 @@
+from contextlib import ExitStack
+
+import concourse.mybir as mybir
+
+K, T, S, N, H = 1024, 2048, 512, 128, 512
+FLOPS = 2 * (2 * K * H * S + H * N * S)
+
+F32 = mybir.dt.float32
+BF16 = mybir.dt.bfloat16
+I32 = mybir.dt.int32
+U32 = mybir.dt.uint32
+U16 = mybir.dt.uint16
+U8 = mybir.dt.uint8
+FP8X4 = mybir.dt.float8_e4m3fn_x4
+COPY = mybir.ActivationFunctionType.Copy
+ADD = mybir.AluOpType.add
+MULT = mybir.AluOpType.mult
+
+P = 128
+PACK = 4
+K_PASS = P * PACK
+PASSES = K // K_PASS
+HALF = S // 2
+CHUNK = 128
+CHUNKS = S // CHUNK
+LIST_COLS = S // 16
+
+
+def tile_picked_ycallgr_two_p_kernel(tc, x_words, x_scales, w1, w2, unit, w3, offs, cle, cr2, out):
+    nc = tc.nc
+    with ExitStack() as ctx:
+        keep = ctx.enter_context(tc.tile_pool(name="keep", bufs=1))
+        psum = ctx.enter_context(tc.psum_pool(name="psum", bufs=1))
+
+        def tile(shape, dtype, name):
+            return keep.tile(shape, dtype, name=name, align_bytes=64)
+
+        offs_sb = keep.tile([P, LIST_COLS], U16, name="offs_sb")
+        cle_sb = keep.tile([P, LIST_COLS], U16, name="cle_sb")
+        cr2_sb = keep.tile([P, LIST_COLS], U16, name="cr2_sb")
+
+        def half_list(list_sb, h):
+            return list_sb[:, h * LIST_COLS // 2 : (h + 1) * LIST_COLS // 2]
+
+        def load_weight(w, o, name):
+            raw = tile([P, PACK, w.shape[1]], F32, name)
+            nc.sync.dma_start(out=raw[:], in_=w[o * K_PASS : (o + 1) * K_PASS, :].rearrange("(p j) c -> p j c", j=PACK))
+            return raw
+
+        def load_words(o):
+            table = tile([P, T], U32, f"x_table{o}")
+            nc.sync.dma_start(out=table[:].bitcast(I32), in_=x_words[o].rearrange("p n t -> p (n t)").bitcast(I32))
+            return table
+
+        scale_table = tile([P, T], U8, "scale_table")
+        nc.vector.memset(scale_table[:].bitcast(I32), 0)
+        w2_raw = [load_weight(w2, 0, "w2_raw0")]
+        nc.sync.dma_start(out=offs_sb[:], in_=offs)
+        for q in range(4):
+            nc.sync.dma_start(
+                out=scale_table[32 * q : 32 * q + 8, :].bitcast(I32),
+                in_=x_scales[:, 4 * q : 4 * q + 4, :].bitcast(I32),
+            )
+        w2_raw.append(load_weight(w2, 1, "w2_raw1"))
+        x_table = [load_words(o) for o in range(PASSES)]
+        unit_sb = tile([P, PACK], F32, "unit_sb")
+        nc.sync.dma_start(out=unit_sb[:], in_=unit.rearrange("(p t) o -> p (t o)", t=PACK))
+        nc.sync.dma_start(out=cle_sb[:], in_=cle)
+        w1_raw = [load_weight(w1, o, f"w1_raw{o}") for o in range(PASSES)]
+        w3_raw = load_weight(w3, 0, "w3_raw")
+        nc.sync.dma_start(out=cr2_sb[:], in_=cr2)
+
+        def deal(raw, name, scalar_share):
+            dealt = tile([P, PACK * H], BF16, name)
+            dst = dealt[:].rearrange("p (t m j) -> p m j t", t=PACK, j=PACK)
+            src = raw[:].rearrange("p j (m t) -> p m j t", t=PACK)
+            cut = P - scalar_share
+            if cut > 0:
+                nc.vector.tensor_copy(out=dst[:, :cut], in_=src[:, :cut])
+            if scalar_share > 0:
+                nc.scalar.copy(out=dst[:, cut:], in_=src[:, cut:])
+            return dealt
+
+        def quantize(values, name):
+            width = values.shape[1] // PACK
+            codes = tile([P, width], U32, name + "_codes")
+            scales = tile([P, width], U8, name + "_scales")
+            nc.vector.quantize_mx(out=codes[:].bitcast(FP8X4), scales=scales[:], in_=values[:])
+            return codes, scales
+
+        x_scale = tile([P, S], U8, "x_scale")
+        nc.vector.tensor_copy(out=x_scale[:], in_=scale_table[:].indirect(offs_sb[:]))
+
+        w2_mx = []
+        for o in range(PASSES):
+            w2_mx.append(quantize(deal(w2_raw[o], f"w2_bf{o}", 32), f"w2_{o}"))
+
+        x_codes = [tile([P, S], U32, f"x_codes{o}") for o in range(PASSES)]
+        nc.vector.tensor_copy(out=x_codes[0][:], in_=x_table[0][:].indirect(offs_sb[:]))
+
+        def product(acc, w_mx, o, t, cols, start, stop):
+            codes, scales = w_mx[o]
+            rows = slice(t * P, (t + 1) * P)
+            nc.tensor.matmul_mx(
+                out=acc,
+                lhsT=codes[:, rows].bitcast(FP8X4),
+                lhsT_scale=scales[:, rows],
+                rhs=x_codes[o][:, cols].bitcast(FP8X4),
+                rhs_scale=x_scale[4 * o :, cols],
+                start=start,
+                stop=stop,
+            )
+
+        z_bank = [psum.tile([P, S], F32, name=f"z_bank{t}", tag=f"bank{t}") for t in range(PACK)]
+        for t in range(PACK):
+            product(z_bank[t][:], w2_mx, 0, t, slice(0, S), True, False)
+
+        u_z = tile([P, PACK], F32, "u_z")
+        u_y = tile([P, PACK], F32, "u_y")
+        nc.vector.tensor_scalar(out=u_z[:], in0=unit_sb[:], scalar1=0.7, scalar2=None, op0=MULT)
+        nc.vector.tensor_scalar(out=u_y[:], in0=unit_sb[:], scalar1=2.0, scalar2=None, op0=MULT)
+
+        for h in range(2):
+            cols = slice(h * HALF, (h + 1) * HALF)
+            nc.vector.tensor_copy(out=x_codes[1][:, cols], in_=x_table[1][:].indirect(half_list(offs_sb, h)))
+            for t in range(PACK):
+                product(z_bank[t][:, cols], w2_mx, 1, t, cols, False, h == 1)
+
+        z_rows = [tile([P, S], F32, f"z_rows{t}") for t in range(PACK)]
+        for t in range(PACK):
+            if t == 1:
+                nc.vector.tensor_scalar(out=z_rows[t][:], in0=z_bank[t][:], scalar1=u_z[:, t : t + 1], scalar2=None, op0=MULT)
+            else:
+                nc.scalar.activation(out=z_rows[t][:], in_=z_bank[t][:], func=COPY, scale=u_z[:, t : t + 1])
+
+        z_picked = tile([P, PACK, S], F32, "z_picked")
+
+        def pick_z(t, h, on_vector):
+            cols = slice(h * HALF, (h + 1) * HALF)
+            window = z_rows[t][:].indirect(half_list(cle_sb, h))
+            if on_vector:
+                nc.vector.tensor_copy(out=z_picked[:, t, cols], in_=window)
+            else:
+                nc.scalar.activation(out=z_picked[:, t, cols], in_=window, func=COPY)
+
+        for h in range(2):
+            for t in (0, 2, 3):
+                pick_z(t, h, False)
+
+        y_bank = [psum.tile([P, PACK, CHUNK], F32, name=f"y_bank{c}", tag=f"bank{PACK + c}") for c in range(CHUNKS)]
+        w1_mx = []
+        for o in range(PASSES):
+            w1_mx.append(quantize(deal(w1_raw[o], f"w1_bf{o}", 0), f"w1_{o}"))
+            for c in range(CHUNKS):
+                for t in range(PACK):
+                    product(y_bank[c][:, t, :], w1_mx, o, t, slice(c * CHUNK, (c + 1) * CHUNK),
+                            o == 0 and t == 0, o == PASSES - 1 and t == PACK - 1)
+
+        for h in range(2):
+            pick_z(1, h, True)
+
+        w3_bf = tile([P, PACK * N], BF16, "w3_bf")
+        nc.vector.tensor_copy(
+            out=w3_bf[:].rearrange("p (c i j) -> p c j i", i=4, j=PACK),
+            in_=w3_raw[:].rearrange("p j (c i) -> p c j i", i=4),
+        )
+        w3_codes, w3_scales = quantize(w3_bf, "w3")
+
+        product_rows = tile([P, S], F32, "product_rows")
+        hid_bf = []
+        for c in range(CHUNKS):
+            cols = slice(c * CHUNK, (c + 1) * CHUNK)
+            y_rows = tile([P, PACK, CHUNK], F32, f"y_rows{c}")
+            for t in range(PACK):
+                nc.scalar.activation(out=y_rows[:, t, :], in_=y_bank[c][:, t, :], func=COPY, scale=u_y[:, t : t + 1])
+            hid = tile([P, PACK * CHUNK], BF16, f"hid{c}")
+            nc.vector.tensor_tensor(
+                out=hid[:].rearrange("p (c i t) -> p c t i", i=4, t=PACK),
+                in0=y_rows[:].rearrange("p t (c i) -> p c t i", i=4),
+                in1=z_picked[:, :, cols].rearrange("p t (c i) -> p c t i", i=4),
+                op=ADD,
+            )
+            hid_bf.append(hid)
+        for c in range(CHUNKS):
+            cols = slice(c * CHUNK, (c + 1) * CHUNK)
+            hid_codes, hid_scales = quantize(hid_bf[c], f"hid{c}")
+            out_bank = psum.tile([P, CHUNK], F32, name=f"out_bank{c}", tag=f"bank{c}")
+            nc.tensor.matmul_mx(
+                out=out_bank[:],
+                lhsT=w3_codes[:].bitcast(FP8X4),
+                lhsT_scale=w3_scales[:],
+                rhs=hid_codes[:].bitcast(FP8X4),
+                rhs_scale=hid_scales[:],
+                start=True,
+                stop=True,
+            )
+            nc.scalar.copy(out=product_rows[:, cols], in_=out_bank[:])
+
+        for h in range(2):
+            cols = slice(h * HALF, (h + 1) * HALF)
+            result = tile([P, HALF], F32, f"result{h}")
+            window = product_rows[:].indirect(half_list(cr2_sb, h))
+            if h == 0:
+                nc.vector.tensor_copy(out=result[:], in_=window)
+                nc.sync.dma_start(out=out[:, cols], in_=result[:])
+            else:
+                nc.scalar.activation(out=result[:], in_=window, func=COPY)
+                nc.scalar.dma_start(out=out[:, cols], in_=result[:])

@@ -53,7 +53,8 @@ def tile_picked_ycallgr_two_p_kernel(tc, x_words, x_scales, w1, w2, unit, w3, of
             return table
 
         scale_table = tile([P, T], U8, "scale_table")
-        nc.vector.memset(scale_table[:].bitcast(I32), 0)
+        nc.gpsimd.memset(scale_table[:, : T // 2].bitcast(I32), 0)
+        nc.vector.memset(scale_table[:, T // 2 :].bitcast(I32), 0)
         w2_raw = [load_weight(w2, 0, "w2_raw0")]
         nc.sync.dma_start(out=offs_sb[:], in_=offs)
         for q in range(4):
@@ -61,11 +62,12 @@ def tile_picked_ycallgr_two_p_kernel(tc, x_words, x_scales, w1, w2, unit, w3, of
                 out=scale_table[32 * q : 32 * q + 8, :].bitcast(I32),
                 in_=x_scales[:, 4 * q : 4 * q + 4, :].bitcast(I32),
             )
+        x_table = [load_words(0)]
         w2_raw.append(load_weight(w2, 1, "w2_raw1"))
-        x_table = [load_words(o) for o in range(PASSES)]
+        x_table.append(load_words(1))
+        nc.sync.dma_start(out=cle_sb[:], in_=cle)
         unit_sb = tile([P, PACK], F32, "unit_sb")
         nc.sync.dma_start(out=unit_sb[:], in_=unit.rearrange("(p t) o -> p (t o)", t=PACK))
-        nc.sync.dma_start(out=cle_sb[:], in_=cle)
         w1_raw = [load_weight(w1, o, f"w1_raw{o}") for o in range(PASSES)]
         w3_raw = load_weight(w3, 0, "w3_raw")
         nc.sync.dma_start(out=cr2_sb[:], in_=cr2)
@@ -85,18 +87,16 @@ def tile_picked_ycallgr_two_p_kernel(tc, x_words, x_scales, w1, w2, unit, w3, of
             width = values.shape[1] // PACK
             codes = tile([P, width], U32, name + "_codes")
             scales = tile([P, width], U8, name + "_scales")
-            nc.vector.quantize_mx(out=codes[:].bitcast(FP8X4), scales=scales[:], in_=values[:])
+            nc.vector.quantize_mx(out=codes[:].bitcast(FP8X4), scales=scales[:], in_=values)
             return codes, scales
 
         x_scale = tile([P, S], U8, "x_scale")
         nc.vector.tensor_copy(out=x_scale[:], in_=scale_table[:].indirect(offs_sb[:]))
 
-        w2_mx = []
-        for o in range(PASSES):
-            w2_mx.append(quantize(deal(w2_raw[o], f"w2_bf{o}", 32), f"w2_{o}"))
-
+        w2_mx = [quantize(deal(w2_raw[0], "w2_bf0", 32)[:], "w2_0")]
         x_codes = [tile([P, S], U32, f"x_codes{o}") for o in range(PASSES)]
         nc.vector.tensor_copy(out=x_codes[0][:], in_=x_table[0][:].indirect(offs_sb[:]))
+        w2_mx.append(quantize(deal(w2_raw[1], "w2_bf1", 64)[:], "w2_1"))
 
         def product(acc, w_mx, o, t, cols, start, stop):
             codes, scales = w_mx[o]
@@ -115,10 +115,8 @@ def tile_picked_ycallgr_two_p_kernel(tc, x_words, x_scales, w1, w2, unit, w3, of
         for t in range(PACK):
             product(z_bank[t][:], w2_mx, 0, t, slice(0, S), True, False)
 
-        u_z = tile([P, PACK], F32, "u_z")
         u_y = tile([P, PACK], F32, "u_y")
-        nc.vector.tensor_scalar(out=u_z[:], in0=unit_sb[:], scalar1=0.7, scalar2=None, op0=MULT)
-        nc.vector.tensor_scalar(out=u_y[:], in0=unit_sb[:], scalar1=2.0, scalar2=None, op0=MULT)
+        nc.gpsimd.tensor_scalar(out=u_y[:], in0=unit_sb[:], scalar1=2.0, scalar2=None, op0=MULT)
 
         for h in range(2):
             cols = slice(h * HALF, (h + 1) * HALF)
@@ -129,62 +127,54 @@ def tile_picked_ycallgr_two_p_kernel(tc, x_words, x_scales, w1, w2, unit, w3, of
         z_rows = [tile([P, S], F32, f"z_rows{t}") for t in range(PACK)]
         for t in range(PACK):
             if t == 1:
-                nc.vector.tensor_scalar(out=z_rows[t][:], in0=z_bank[t][:], scalar1=u_z[:, t : t + 1], scalar2=None, op0=MULT)
+                nc.vector.tensor_scalar(out=z_rows[t][:], in0=z_bank[t][:], scalar1=unit_sb[:, t : t + 1], scalar2=None, op0=MULT)
             else:
-                nc.scalar.activation(out=z_rows[t][:], in_=z_bank[t][:], func=COPY, scale=u_z[:, t : t + 1])
+                nc.scalar.activation(out=z_rows[t][:], in_=z_bank[t][:], func=COPY, scale=unit_sb[:, t : t + 1])
 
-        z_picked = tile([P, PACK, S], F32, "z_picked")
-
-        def pick_z(t, h, on_vector):
+        z_picked = [tile([P, S], F32, f"z_picked{t}") for t in range(PACK)]
+        for h in range(2):
             cols = slice(h * HALF, (h + 1) * HALF)
-            window = z_rows[t][:].indirect(half_list(cle_sb, h))
-            if on_vector:
-                nc.vector.tensor_copy(out=z_picked[:, t, cols], in_=window)
-            else:
-                nc.scalar.activation(out=z_picked[:, t, cols], in_=window, func=COPY)
+            for t in range(PACK):
+                nc.scalar.activation(out=z_picked[t][:, cols], in_=z_rows[t][:].indirect(half_list(cle_sb, h)), func=COPY, scale=0.7)
 
-        for h in range(2):
-            for t in (0, 2, 3):
-                pick_z(t, h, False)
+        y_bank = [psum.tile([P, S], F32, name=f"y_bank{t}", tag=f"bank{PACK + t}") for t in range(PACK)]
+        w1_mx = [quantize(deal(w1_raw[0], "w1_bf0", 0)[:], "w1_0")]
+        for t in range(PACK):
+            product(y_bank[t][:], w1_mx, 0, t, slice(0, S), True, False)
+        w1_last = deal(w1_raw[1], "w1_bf1", 0)
+        for t in range(PACK):
+            codes, scales = quantize(w1_last[:, t * K_PASS : (t + 1) * K_PASS], f"w1_1_{t}")
+            nc.tensor.matmul_mx(
+                out=y_bank[t][:],
+                lhsT=codes[:].bitcast(FP8X4),
+                lhsT_scale=scales[:],
+                rhs=x_codes[1][:].bitcast(FP8X4),
+                rhs_scale=x_scale[4:, :],
+                start=False,
+                stop=True,
+            )
 
-        y_bank = [psum.tile([P, PACK, CHUNK], F32, name=f"y_bank{c}", tag=f"bank{PACK + c}") for c in range(CHUNKS)]
-        w1_mx = []
-        for o in range(PASSES):
-            w1_mx.append(quantize(deal(w1_raw[o], f"w1_bf{o}", 0), f"w1_{o}"))
-            for c in range(CHUNKS):
-                for t in range(PACK):
-                    product(y_bank[c][:, t, :], w1_mx, o, t, slice(c * CHUNK, (c + 1) * CHUNK),
-                            o == 0 and t == 0, o == PASSES - 1 and t == PACK - 1)
+        hid_rows = [tile([P, PACK, HALF], BF16, f"hid_rows{h}") for h in range(2)]
+        hid_bf = [tile([P, PACK * HALF], BF16, f"hid_bf{h}") for h in range(2)]
 
-        for h in range(2):
-            pick_z(1, h, True)
+        def combine(h):
+            cols = slice(h * HALF, (h + 1) * HALF)
+            for t in range(PACK):
+                nc.vector.scalar_tensor_tensor(
+                    out=hid_rows[h][:, t, :], in0=y_bank[t][:, cols], scalar=u_y[:, t : t + 1],
+                    in1=z_picked[t][:, cols], op0=MULT, op1=ADD,
+                )
 
-        w3_bf = tile([P, PACK * N], BF16, "w3_bf")
-        nc.vector.tensor_copy(
-            out=w3_bf[:].rearrange("p (c i j) -> p c j i", i=4, j=PACK),
-            in_=w3_raw[:].rearrange("p j (c i) -> p c j i", i=4),
-        )
-        w3_codes, w3_scales = quantize(w3_bf, "w3")
+        def weave(copy, h, lo, hi):
+            dst = hid_bf[h][:].rearrange("p (c i t) -> p c t i", i=4, t=PACK)
+            src = hid_rows[h][:].rearrange("p t (c i) -> p c t i", i=4)
+            copy(out=dst[:, lo // 4 : hi // 4], in_=src[:, lo // 4 : hi // 4])
 
         product_rows = tile([P, S], F32, "product_rows")
-        hid_bf = []
-        for c in range(CHUNKS):
-            cols = slice(c * CHUNK, (c + 1) * CHUNK)
-            y_rows = tile([P, PACK, CHUNK], F32, f"y_rows{c}")
-            for t in range(PACK):
-                nc.scalar.activation(out=y_rows[:, t, :], in_=y_bank[c][:, t, :], func=COPY, scale=u_y[:, t : t + 1])
-            hid = tile([P, PACK * CHUNK], BF16, f"hid{c}")
-            nc.vector.tensor_tensor(
-                out=hid[:].rearrange("p (c i t) -> p c t i", i=4, t=PACK),
-                in0=y_rows[:].rearrange("p t (c i) -> p c t i", i=4),
-                in1=z_picked[:, :, cols].rearrange("p t (c i) -> p c t i", i=4),
-                op=ADD,
-            )
-            hid_bf.append(hid)
-        for c in range(CHUNKS):
-            cols = slice(c * CHUNK, (c + 1) * CHUNK)
-            hid_codes, hid_scales = quantize(hid_bf[c], f"hid{c}")
-            out_bank = psum.tile([P, CHUNK], F32, name=f"out_bank{c}", tag=f"bank{c}")
+
+        def finish(h):
+            hid_codes, hid_scales = quantize(hid_bf[h][:], f"hid{h}")
+            out_bank = psum.tile([P, HALF], F32, name=f"out_bank{h}", tag=f"bank{h}")
             nc.tensor.matmul_mx(
                 out=out_bank[:],
                 lhsT=w3_codes[:].bitcast(FP8X4),
@@ -194,7 +184,23 @@ def tile_picked_ycallgr_two_p_kernel(tc, x_words, x_scales, w1, w2, unit, w3, of
                 start=True,
                 stop=True,
             )
-            nc.scalar.copy(out=product_rows[:, cols], in_=out_bank[:])
+            return out_bank
+
+        combine(0)
+        weave(nc.scalar.copy, 0, 0, HALF)
+        w3_bf = keep.tile([P, PACK * N], BF16, name="w3_bf", tag="w1_bf1", align_bytes=64)
+        nc.vector.tensor_copy(
+            out=w3_bf[:].rearrange("p (c i j) -> p c j i", i=4, j=PACK),
+            in_=w3_raw[:].rearrange("p j (c i) -> p c j i", i=4),
+        )
+        combine(1)
+        w3_codes, w3_scales = quantize(w3_bf[:], "w3")
+        weave(nc.scalar.copy, 1, HALF // 2, HALF)
+        out_banks = [finish(0)]
+        weave(nc.vector.tensor_copy, 1, 0, HALF // 2)
+        nc.scalar.copy(out=product_rows[:, :HALF], in_=out_banks[0][:])
+        out_banks.append(finish(1))
+        nc.scalar.copy(out=product_rows[:, HALF:], in_=out_banks[1][:])
 
         for h in range(2):
             cols = slice(h * HALF, (h + 1) * HALF)

@@ -20,10 +20,14 @@ P = 128
 PACK = 4
 K_PASS = P * PACK
 PASSES = K // K_PASS
-HALF = S // 2
-CHUNK = 128
-CHUNKS = S // CHUNK
+QUADRANTS = 4
+LINE = 4
 LIST_COLS = S // 16
+HALF = S // 2
+QUARTER = S // 4
+CHUNKS = [(0, HALF), (HALF, HALF + QUARTER), (HALF + QUARTER, S)]
+W2_GROUPS_ON_SCALAR = (32, 64)
+Z_SLOT_ON_VECTOR = 1
 
 
 def tile_picked_ycallgr_two_p_kernel(tc, x_words, x_scales, w1, w2, unit, w3, offs, cle, cr2, out):
@@ -57,9 +61,9 @@ def tile_picked_ycallgr_two_p_kernel(tc, x_words, x_scales, w1, w2, unit, w3, of
         nc.vector.memset(scale_table[:, T // 2 :].bitcast(I32), 0)
         w2_raw = [load_weight(w2, 0, "w2_raw0")]
         nc.sync.dma_start(out=offs_sb[:], in_=offs)
-        for q in range(4):
+        for q in range(QUADRANTS):
             nc.sync.dma_start(
-                out=scale_table[32 * q : 32 * q + 8, :].bitcast(I32),
+                out=scale_table[32 * q : 32 * q + 4 * PASSES, :].bitcast(I32),
                 in_=x_scales[:, 4 * q : 4 * q + 4, :].bitcast(I32),
             )
         x_table = [load_words(0)]
@@ -72,14 +76,13 @@ def tile_picked_ycallgr_two_p_kernel(tc, x_words, x_scales, w1, w2, unit, w3, of
         w3_raw = load_weight(w3, 0, "w3_raw")
         nc.sync.dma_start(out=cr2_sb[:], in_=cr2)
 
-        def deal(raw, name, scalar_share):
+        def deal(raw, name, groups_on_scalar):
             dealt = tile([P, PACK * H], BF16, name)
             dst = dealt[:].rearrange("p (t m j) -> p m j t", t=PACK, j=PACK)
             src = raw[:].rearrange("p j (m t) -> p m j t", t=PACK)
-            cut = P - scalar_share
-            if cut > 0:
-                nc.vector.tensor_copy(out=dst[:, :cut], in_=src[:, :cut])
-            if scalar_share > 0:
+            cut = P - groups_on_scalar
+            nc.vector.tensor_copy(out=dst[:, :cut], in_=src[:, :cut])
+            if groups_on_scalar > 0:
                 nc.scalar.copy(out=dst[:, cut:], in_=src[:, cut:])
             return dealt
 
@@ -90,43 +93,43 @@ def tile_picked_ycallgr_two_p_kernel(tc, x_words, x_scales, w1, w2, unit, w3, of
             nc.vector.quantize_mx(out=codes[:].bitcast(FP8X4), scales=scales[:], in_=values)
             return codes, scales
 
-        x_scale = tile([P, S], U8, "x_scale")
-        nc.vector.tensor_copy(out=x_scale[:], in_=scale_table[:].indirect(offs_sb[:]))
-
-        w2_mx = [quantize(deal(w2_raw[0], "w2_bf0", 32)[:], "w2_0")]
+        w2_mx = [quantize(deal(w2_raw[0], "w2_bf0", W2_GROUPS_ON_SCALAR[0])[:], "w2_0")]
         x_codes = [tile([P, S], U32, f"x_codes{o}") for o in range(PASSES)]
         nc.vector.tensor_copy(out=x_codes[0][:], in_=x_table[0][:].indirect(offs_sb[:]))
-        w2_mx.append(quantize(deal(w2_raw[1], "w2_bf1", 64)[:], "w2_1"))
+        x_scale = tile([P, S], U8, "x_scale")
+        nc.vector.tensor_copy(out=x_scale[:], in_=scale_table[:].indirect(offs_sb[:]))
+        w2_mx.append(quantize(deal(w2_raw[1], "w2_bf1", W2_GROUPS_ON_SCALAR[1])[:], "w2_1"))
 
-        def product(acc, w_mx, o, t, cols, start, stop):
-            codes, scales = w_mx[o]
-            rows = slice(t * P, (t + 1) * P)
+        def x_pass(acc, w_codes, w_scales, o, cols, start, stop):
             nc.tensor.matmul_mx(
                 out=acc,
-                lhsT=codes[:, rows].bitcast(FP8X4),
-                lhsT_scale=scales[:, rows],
+                lhsT=w_codes.bitcast(FP8X4),
+                lhsT_scale=w_scales,
                 rhs=x_codes[o][:, cols].bitcast(FP8X4),
                 rhs_scale=x_scale[4 * o :, cols],
                 start=start,
                 stop=stop,
             )
 
+        def slot(plane, t):
+            return plane[:, t * P : (t + 1) * P]
+
         z_bank = [psum.tile([P, S], F32, name=f"z_bank{t}", tag=f"bank{t}") for t in range(PACK)]
         for t in range(PACK):
-            product(z_bank[t][:], w2_mx, 0, t, slice(0, S), True, False)
+            x_pass(z_bank[t][:], slot(w2_mx[0][0], t), slot(w2_mx[0][1], t), 0, slice(0, S), True, False)
 
-        u_y = tile([P, PACK], F32, "u_y")
-        nc.gpsimd.tensor_scalar(out=u_y[:], in0=unit_sb[:], scalar1=2.0, scalar2=None, op0=MULT)
+        unit_twice = tile([P, PACK], F32, "unit_twice")
+        nc.gpsimd.tensor_scalar(out=unit_twice[:], in0=unit_sb[:], scalar1=2.0, scalar2=None, op0=MULT)
 
         for h in range(2):
             cols = slice(h * HALF, (h + 1) * HALF)
             nc.vector.tensor_copy(out=x_codes[1][:, cols], in_=x_table[1][:].indirect(half_list(offs_sb, h)))
             for t in range(PACK):
-                product(z_bank[t][:, cols], w2_mx, 1, t, cols, False, h == 1)
+                x_pass(z_bank[t][:, cols], slot(w2_mx[1][0], t), slot(w2_mx[1][1], t), 1, cols, False, h == 1)
 
         z_rows = [tile([P, S], F32, f"z_rows{t}") for t in range(PACK)]
         for t in range(PACK):
-            if t == 1:
+            if t == Z_SLOT_ON_VECTOR:
                 nc.vector.tensor_scalar(out=z_rows[t][:], in0=z_bank[t][:], scalar1=unit_sb[:, t : t + 1], scalar2=None, op0=MULT)
             else:
                 nc.scalar.activation(out=z_rows[t][:], in_=z_bank[t][:], func=COPY, scale=unit_sb[:, t : t + 1])
@@ -137,78 +140,93 @@ def tile_picked_ycallgr_two_p_kernel(tc, x_words, x_scales, w1, w2, unit, w3, of
             for t in range(PACK):
                 nc.scalar.activation(out=z_picked[t][:, cols], in_=z_rows[t][:].indirect(half_list(cle_sb, h)), func=COPY, scale=0.7)
 
-        y_bank = [psum.tile([P, S], F32, name=f"y_bank{t}", tag=f"bank{PACK + t}") for t in range(PACK)]
-        w1_mx = [quantize(deal(w1_raw[0], "w1_bf0", 0)[:], "w1_0")]
-        for t in range(PACK):
-            product(y_bank[t][:], w1_mx, 0, t, slice(0, S), True, False)
-        w1_last = deal(w1_raw[1], "w1_bf1", 0)
-        for t in range(PACK):
-            codes, scales = quantize(w1_last[:, t * K_PASS : (t + 1) * K_PASS], f"w1_1_{t}")
-            nc.tensor.matmul_mx(
-                out=y_bank[t][:],
-                lhsT=codes[:].bitcast(FP8X4),
-                lhsT_scale=scales[:],
-                rhs=x_codes[1][:].bitcast(FP8X4),
-                rhs_scale=x_scale[4:, :],
-                start=False,
-                stop=True,
-            )
+        y_bank = [
+            [psum.tile([P, 2, HALF], F32, name=f"y_bank{h}{pair}", tag=f"bank{PACK + 2 * h + pair}") for pair in range(2)]
+            for h in range(2)
+        ]
 
-        hid_rows = [tile([P, PACK, HALF], BF16, f"hid_rows{h}") for h in range(2)]
-        hid_bf = [tile([P, PACK * HALF], BF16, f"hid_bf{h}") for h in range(2)]
+        def y_pass(o, t, w_codes, w_scales, h):
+            start = o == 0 and t % 2 == 0
+            stop = o == PASSES - 1 and t % 2 == 1
+            x_pass(y_bank[h][t // 2][:, t % 2, :], w_codes, w_scales, o, slice(h * HALF, (h + 1) * HALF), start, stop)
 
-        def combine(h):
-            cols = slice(h * HALF, (h + 1) * HALF)
+        w1_first = quantize(deal(w1_raw[0], "w1_bf0", 0)[:], "w1_0")
+        for h in range(2):
             for t in range(PACK):
-                nc.vector.scalar_tensor_tensor(
-                    out=hid_rows[h][:, t, :], in0=y_bank[t][:, cols], scalar=u_y[:, t : t + 1],
-                    in1=z_picked[t][:, cols], op0=MULT, op1=ADD,
-                )
+                y_pass(0, t, slot(w1_first[0], t), slot(w1_first[1], t), h)
+        w1_last_bf = deal(w1_raw[1], "w1_bf1", 0)
 
-        def weave(copy, h, lo, hi):
-            dst = hid_bf[h][:].rearrange("p (c i t) -> p c t i", i=4, t=PACK)
-            src = hid_rows[h][:].rearrange("p t (c i) -> p c t i", i=4)
-            copy(out=dst[:, lo // 4 : hi // 4], in_=src[:, lo // 4 : hi // 4])
+        w3_bf = keep.tile([P, PACK * N], BF16, name="w3_bf", tag="w1_raw1", align_bytes=64)
+        nc.vector.tensor_copy(
+            out=w3_bf[:].rearrange("p (c i j) -> p c j i", i=LINE, j=PACK),
+            in_=w3_raw[:].rearrange("p j (c i) -> p c j i", i=LINE),
+        )
 
+        w1_last = []
+        for t in range(PACK):
+            w1_last.append(quantize(w1_last_bf[:, t * K_PASS : (t + 1) * K_PASS], f"w1_1_{t}"))
+            y_pass(1, t, w1_last[t][0][:], w1_last[t][1][:], 0)
+        for t in range(PACK):
+            y_pass(1, t, w1_last[t][0][:], w1_last[t][1][:], 1)
+        w3_codes, w3_scales = quantize(w3_bf[:], "w3")
+
+        v_slots = [tile([P, PACK, hi - lo], BF16, f"v_slots{lo}") for lo, hi in CHUNKS]
+        v_woven = [tile([P, PACK * (hi - lo)], BF16, f"v_woven{lo}") for lo, hi in CHUNKS]
         product_rows = tile([P, S], F32, "product_rows")
 
-        def finish(h):
-            hid_codes, hid_scales = quantize(hid_bf[h][:], f"hid{h}")
-            out_bank = psum.tile([P, HALF], F32, name=f"out_bank{h}", tag=f"bank{h}")
+        def combine(chunk):
+            lo, hi = CHUNKS[chunk]
+            h = lo // HALF
+            for t in range(PACK):
+                nc.vector.scalar_tensor_tensor(
+                    out=v_slots[chunk][:, t, :],
+                    in0=y_bank[h][t // 2][:, t % 2, lo - h * HALF : hi - h * HALF],
+                    scalar=unit_twice[:, t : t + 1],
+                    in1=z_picked[t][:, lo:hi],
+                    op0=MULT,
+                    op1=ADD,
+                )
+
+        def weave_on_scalar(chunk, lo, hi):
+            dst = v_woven[chunk][:].rearrange("p (c i t) -> p c t i", i=LINE, t=PACK)
+            src = v_slots[chunk][:].rearrange("p t (c i) -> p c t i", i=LINE)
+            nc.scalar.copy(out=dst[:, lo // LINE : hi // LINE], in_=src[:, lo // LINE : hi // LINE])
+
+        def last_product(chunk):
+            lo, hi = CHUNKS[chunk]
+            v_codes, v_scales = quantize(v_woven[chunk][:], f"v{chunk}")
+            out_bank = psum.tile([P, hi - lo], F32, name=f"out_bank{chunk}", tag=f"bank{chunk}")
             nc.tensor.matmul_mx(
                 out=out_bank[:],
                 lhsT=w3_codes[:].bitcast(FP8X4),
                 lhsT_scale=w3_scales[:],
-                rhs=hid_codes[:].bitcast(FP8X4),
-                rhs_scale=hid_scales[:],
+                rhs=v_codes[:].bitcast(FP8X4),
+                rhs_scale=v_scales[:],
                 start=True,
                 stop=True,
             )
             return out_bank
 
         combine(0)
-        weave(nc.scalar.copy, 0, 0, HALF)
-        w3_bf = keep.tile([P, PACK * N], BF16, name="w3_bf", tag="w1_bf1", align_bytes=64)
-        nc.vector.tensor_copy(
-            out=w3_bf[:].rearrange("p (c i j) -> p c j i", i=4, j=PACK),
-            in_=w3_raw[:].rearrange("p j (c i) -> p c j i", i=4),
+        nc.gpsimd.tensor_scalar(
+            out=v_woven[0][:, : PACK * QUARTER].rearrange("p (n t) -> p n t", t=PACK),
+            in0=v_slots[0][:, :, :QUARTER].rearrange("p t n -> p n t"),
+            scalar1=1.0,
+            scalar2=0.0,
+            op0=MULT,
+            op1=ADD,
         )
-        combine(1)
-        w3_codes, w3_scales = quantize(w3_bf[:], "w3")
-        weave(nc.scalar.copy, 1, HALF // 2, HALF)
-        out_banks = [finish(0)]
-        weave(nc.vector.tensor_copy, 1, 0, HALF // 2)
-        nc.scalar.copy(out=product_rows[:, :HALF], in_=out_banks[0][:])
-        out_banks.append(finish(1))
-        nc.scalar.copy(out=product_rows[:, HALF:], in_=out_banks[1][:])
+        weave_on_scalar(0, QUARTER, HALF)
+        for chunk in range(1, len(CHUNKS)):
+            combine(chunk)
+            weave_on_scalar(chunk, 0, QUARTER)
+        out_banks = [last_product(chunk) for chunk in range(len(CHUNKS))]
+        nc.vector.tensor_copy(out=product_rows[:, :HALF], in_=out_banks[0][:])
+        for chunk in range(1, len(CHUNKS)):
+            nc.scalar.copy(out=product_rows[:, CHUNKS[chunk][0] : CHUNKS[chunk][1]], in_=out_banks[chunk][:])
 
-        for h in range(2):
-            cols = slice(h * HALF, (h + 1) * HALF)
-            result = tile([P, HALF], F32, f"result{h}")
-            window = product_rows[:].indirect(half_list(cr2_sb, h))
-            if h == 0:
-                nc.vector.tensor_copy(out=result[:], in_=window)
-                nc.sync.dma_start(out=out[:, cols], in_=result[:])
-            else:
-                nc.scalar.activation(out=result[:], in_=window, func=COPY)
-                nc.scalar.dma_start(out=out[:, cols], in_=result[:])
+        result = [tile([P, HALF], F32, f"result{h}") for h in range(2)]
+        nc.vector.tensor_copy(out=result[0][:], in_=product_rows[:].indirect(half_list(cr2_sb, 0)))
+        nc.sync.dma_start(out=out[:, :HALF], in_=result[0][:])
+        nc.scalar.activation(out=result[1][:], in_=product_rows[:].indirect(half_list(cr2_sb, 1)), func=COPY)
+        nc.scalar.dma_start(out=out[:, HALF:], in_=result[1][:])

from contextlib import ExitStack

import concourse.mybir as mybir

K, T, S, N, H = 1024, 2048, 512, 128, 512
FLOPS = 2 * (2 * K * H * S + H * N * S)

F32 = mybir.dt.float32
BF16 = mybir.dt.bfloat16
I32 = mybir.dt.int32
U32 = mybir.dt.uint32
U16 = mybir.dt.uint16
U8 = mybir.dt.uint8
FP8X4 = mybir.dt.float8_e4m3fn_x4
COPY = mybir.ActivationFunctionType.Copy
ADD = mybir.AluOpType.add
MULT = mybir.AluOpType.mult

P = 128
PACK = 4
K_PASS = P * PACK
PASSES = K // K_PASS
QUADRANTS = 4
LINE = 4
LIST_COLS = S // 16
HALF = S // 2
QUARTER = S // 4
CHUNKS = [(0, HALF), (HALF, HALF + QUARTER), (HALF + QUARTER, S)]
W2_GROUPS_ON_SCALAR = (32, 64)
Z_SLOT_ON_VECTOR = 1


def tile_picked_ycallgr_two_p_kernel(tc, x_words, x_scales, w1, w2, unit, w3, offs, cle, cr2, out):
    nc = tc.nc
    with ExitStack() as ctx:
        keep = ctx.enter_context(tc.tile_pool(name="keep", bufs=1))
        psum = ctx.enter_context(tc.psum_pool(name="psum", bufs=1))

        def tile(shape, dtype, name):
            return keep.tile(shape, dtype, name=name, align_bytes=64)

        offs_sb = keep.tile([P, LIST_COLS], U16, name="offs_sb")
        cle_sb = keep.tile([P, LIST_COLS], U16, name="cle_sb")
        cr2_sb = keep.tile([P, LIST_COLS], U16, name="cr2_sb")

        def half_list(list_sb, h):
            return list_sb[:, h * LIST_COLS // 2 : (h + 1) * LIST_COLS // 2]

        def load_weight(w, o, name):
            raw = tile([P, PACK, w.shape[1]], F32, name)
            nc.sync.dma_start(out=raw[:], in_=w[o * K_PASS : (o + 1) * K_PASS, :].rearrange("(p j) c -> p j c", j=PACK))
            return raw

        def load_words(o):
            table = tile([P, T], U32, f"x_table{o}")
            nc.sync.dma_start(out=table[:].bitcast(I32), in_=x_words[o].rearrange("p n t -> p (n t)").bitcast(I32))
            return table

        scale_table = tile([P, T], U8, "scale_table")
        nc.gpsimd.memset(scale_table[:, : T // 2].bitcast(I32), 0)
        nc.vector.memset(scale_table[:, T // 2 :].bitcast(I32), 0)
        w2_raw = [load_weight(w2, 0, "w2_raw0")]
        nc.sync.dma_start(out=offs_sb[:], in_=offs)
        for q in range(QUADRANTS):
            nc.sync.dma_start(
                out=scale_table[32 * q : 32 * q + 4 * PASSES, :].bitcast(I32),
                in_=x_scales[:, 4 * q : 4 * q + 4, :].bitcast(I32),
            )
        x_table = [load_words(0)]
        w2_raw.append(load_weight(w2, 1, "w2_raw1"))
        x_table.append(load_words(1))
        nc.sync.dma_start(out=cle_sb[:], in_=cle)
        unit_sb = tile([P, PACK], F32, "unit_sb")
        nc.sync.dma_start(out=unit_sb[:], in_=unit.rearrange("(p t) o -> p (t o)", t=PACK))
        w1_raw = [load_weight(w1, o, f"w1_raw{o}") for o in range(PASSES)]
        w3_raw = load_weight(w3, 0, "w3_raw")
        nc.sync.dma_start(out=cr2_sb[:], in_=cr2)

        def deal(raw, name, groups_on_scalar):
            dealt = tile([P, PACK * H], BF16, name)
            dst = dealt[:].rearrange("p (t m j) -> p m j t", t=PACK, j=PACK)
            src = raw[:].rearrange("p j (m t) -> p m j t", t=PACK)
            cut = P - groups_on_scalar
            nc.vector.tensor_copy(out=dst[:, :cut], in_=src[:, :cut])
            if groups_on_scalar > 0:
                nc.scalar.copy(out=dst[:, cut:], in_=src[:, cut:])
            return dealt

        def quantize(values, name):
            width = values.shape[1] // PACK
            codes = tile([P, width], U32, name + "_codes")
            scales = tile([P, width], U8, name + "_scales")
            nc.vector.quantize_mx(out=codes[:].bitcast(FP8X4), scales=scales[:], in_=values)
            return codes, scales

        w2_mx = [quantize(deal(w2_raw[0], "w2_bf0", W2_GROUPS_ON_SCALAR[0])[:], "w2_0")]
        x_codes = [tile([P, S], U32, f"x_codes{o}") for o in range(PASSES)]
        nc.vector.tensor_copy(out=x_codes[0][:], in_=x_table[0][:].indirect(offs_sb[:]))
        x_scale = tile([P, S], U8, "x_scale")
        nc.vector.tensor_copy(out=x_scale[:], in_=scale_table[:].indirect(offs_sb[:]))
        w2_mx.append(quantize(deal(w2_raw[1], "w2_bf1", W2_GROUPS_ON_SCALAR[1])[:], "w2_1"))

        def x_pass(acc, w_codes, w_scales, o, cols, start, stop):
            nc.tensor.matmul_mx(
                out=acc,
                lhsT=w_codes.bitcast(FP8X4),
                lhsT_scale=w_scales,
                rhs=x_codes[o][:, cols].bitcast(FP8X4),
                rhs_scale=x_scale[4 * o :, cols],
                start=start,
                stop=stop,
            )

        def slot(plane, t):
            return plane[:, t * P : (t + 1) * P]

        z_bank = [psum.tile([P, S], F32, name=f"z_bank{t}", tag=f"bank{t}") for t in range(PACK)]
        for t in range(PACK):
            x_pass(z_bank[t][:], slot(w2_mx[0][0], t), slot(w2_mx[0][1], t), 0, slice(0, S), True, False)

        unit_twice = tile([P, PACK], F32, "unit_twice")
        nc.gpsimd.tensor_scalar(out=unit_twice[:], in0=unit_sb[:], scalar1=2.0, scalar2=None, op0=MULT)

        for h in range(2):
            cols = slice(h * HALF, (h + 1) * HALF)
            nc.vector.tensor_copy(out=x_codes[1][:, cols], in_=x_table[1][:].indirect(half_list(offs_sb, h)))
            for t in range(PACK):
                x_pass(z_bank[t][:, cols], slot(w2_mx[1][0], t), slot(w2_mx[1][1], t), 1, cols, False, h == 1)

        z_rows = [tile([P, S], F32, f"z_rows{t}") for t in range(PACK)]
        for t in range(PACK):
            if t == Z_SLOT_ON_VECTOR:
                nc.vector.tensor_scalar(out=z_rows[t][:], in0=z_bank[t][:], scalar1=unit_sb[:, t : t + 1], scalar2=None, op0=MULT)
            else:
                nc.scalar.activation(out=z_rows[t][:], in_=z_bank[t][:], func=COPY, scale=unit_sb[:, t : t + 1])

        z_picked = [tile([P, S], F32, f"z_picked{t}") for t in range(PACK)]
        for h in range(2):
            cols = slice(h * HALF, (h + 1) * HALF)
            for t in range(PACK):
                nc.scalar.activation(out=z_picked[t][:, cols], in_=z_rows[t][:].indirect(half_list(cle_sb, h)), func=COPY, scale=0.7)

        y_bank = [
            [psum.tile([P, 2, HALF], F32, name=f"y_bank{h}{pair}", tag=f"bank{PACK + 2 * h + pair}") for pair in range(2)]
            for h in range(2)
        ]

        def y_pass(o, t, w_codes, w_scales, h):
            start = o == 0 and t % 2 == 0
            stop = o == PASSES - 1 and t % 2 == 1
            x_pass(y_bank[h][t // 2][:, t % 2, :], w_codes, w_scales, o, slice(h * HALF, (h + 1) * HALF), start, stop)

        w1_first = quantize(deal(w1_raw[0], "w1_bf0", 0)[:], "w1_0")
        for h in range(2):
            for t in range(PACK):
                y_pass(0, t, slot(w1_first[0], t), slot(w1_first[1], t), h)
        w1_last_bf = deal(w1_raw[1], "w1_bf1", 0)

        w3_bf = keep.tile([P, PACK * N], BF16, name="w3_bf", tag="w1_raw1", align_bytes=64)
        nc.vector.tensor_copy(
            out=w3_bf[:].rearrange("p (c i j) -> p c j i", i=LINE, j=PACK),
            in_=w3_raw[:].rearrange("p j (c i) -> p c j i", i=LINE),
        )

        w1_last = []
        for t in range(PACK):
            w1_last.append(quantize(w1_last_bf[:, t * K_PASS : (t + 1) * K_PASS], f"w1_1_{t}"))
            y_pass(1, t, w1_last[t][0][:], w1_last[t][1][:], 0)
        for t in range(PACK):
            y_pass(1, t, w1_last[t][0][:], w1_last[t][1][:], 1)
        w3_codes, w3_scales = quantize(w3_bf[:], "w3")

        v_slots = [tile([P, PACK, hi - lo], BF16, f"v_slots{lo}") for lo, hi in CHUNKS]
        v_woven = [tile([P, PACK * (hi - lo)], BF16, f"v_woven{lo}") for lo, hi in CHUNKS]
        product_rows = tile([P, S], F32, "product_rows")

        def combine(chunk):
            lo, hi = CHUNKS[chunk]
            h = lo // HALF
            for t in range(PACK):
                nc.vector.scalar_tensor_tensor(
                    out=v_slots[chunk][:, t, :],
                    in0=y_bank[h][t // 2][:, t % 2, lo - h * HALF : hi - h * HALF],
                    scalar=unit_twice[:, t : t + 1],
                    in1=z_picked[t][:, lo:hi],
                    op0=MULT,
                    op1=ADD,
                )

        def weave_on_scalar(chunk, lo, hi):
            dst = v_woven[chunk][:].rearrange("p (c i t) -> p c t i", i=LINE, t=PACK)
            src = v_slots[chunk][:].rearrange("p t (c i) -> p c t i", i=LINE)
            nc.scalar.copy(out=dst[:, lo // LINE : hi // LINE], in_=src[:, lo // LINE : hi // LINE])

        def last_product(chunk):
            lo, hi = CHUNKS[chunk]
            v_codes, v_scales = quantize(v_woven[chunk][:], f"v{chunk}")
            out_bank = psum.tile([P, hi - lo], F32, name=f"out_bank{chunk}", tag=f"bank{chunk}")
            nc.tensor.matmul_mx(
                out=out_bank[:],
                lhsT=w3_codes[:].bitcast(FP8X4),
                lhsT_scale=w3_scales[:],
                rhs=v_codes[:].bitcast(FP8X4),
                rhs_scale=v_scales[:],
                start=True,
                stop=True,
            )
            return out_bank

        combine(0)
        nc.gpsimd.tensor_scalar(
            out=v_woven[0][:, : PACK * QUARTER].rearrange("p (n t) -> p n t", t=PACK),
            in0=v_slots[0][:, :, :QUARTER].rearrange("p t n -> p n t"),
            scalar1=1.0,
            scalar2=0.0,
            op0=MULT,
            op1=ADD,
        )
        weave_on_scalar(0, QUARTER, HALF)
        for chunk in range(1, len(CHUNKS)):
            combine(chunk)
            weave_on_scalar(chunk, 0, QUARTER)
        out_banks = [last_product(chunk) for chunk in range(len(CHUNKS))]
        nc.vector.tensor_copy(out=product_rows[:, :HALF], in_=out_banks[0][:])
        for chunk in range(1, len(CHUNKS)):
            nc.scalar.copy(out=product_rows[:, CHUNKS[chunk][0] : CHUNKS[chunk][1]], in_=out_banks[chunk][:])

        result = [tile([P, HALF], F32, f"result{h}") for h in range(2)]
        nc.vector.tensor_copy(out=result[0][:], in_=product_rows[:].indirect(half_list(cr2_sb, 0)))
        nc.sync.dma_start(out=out[:, :HALF], in_=result[0][:])
        nc.scalar.activation(out=result[1][:], in_=product_rows[:].indirect(half_list(cr2_sb, 1)), func=COPY)
        nc.scalar.dma_start(out=out[:, HALF:], in_=result[1][:])
